import numpy as np
import ml_dtypes


def mxq(x, axis, fmt="e4m3"):
    dtype, down = {"e4m3": (ml_dtypes.float8_e4m3fn, 7), "e5m2": (ml_dtypes.float8_e5m2, 14)}[fmt]
    v = np.moveaxis(np.asarray(x, np.float32).astype(ml_dtypes.bfloat16).astype(np.float64), axis, -1)
    blocks = v.reshape(v.shape[:-1] + (-1, 32))
    amax = np.abs(blocks).max(-1, keepdims=True)
    byte = np.maximum(np.where(amax > 0, np.frexp(amax)[1] - 1 + 127, 0) - down, 1)
    scale = np.exp2(byte - 127.0)
    codes = (blocks / scale).astype(np.float32).astype(dtype).astype(np.float64)
    return np.moveaxis((codes * scale).reshape(v.shape), -1, axis)


WIDE = False


def mx_kscale(k):
    if not WIDE:
        return np.ones(k)
    levels = np.array([10, -10, 5, -5, 0])
    if k % 512:
        return np.exp2(np.random.permutation(np.resize(levels, k // 32))).repeat(32)
    a = np.empty((k // 512, 16))
    for p in range(k // 512):
        a[p, :8] = np.random.permutation(np.resize(levels, 8))
        for g in range(8):
            far = levels[np.abs(levels - a[p, g]) >= 10]
            a[p, g + 8] = far[np.random.randint(len(far))]
    return np.exp2(a.ravel()).repeat(32)


def f64(x):
    return np.asarray(x).astype(np.float64)


def striped(idx):
    return np.tile(idx.reshape(-1, 16).T, (8, 1)).astype(np.uint16)


def unstriped(offs):
    return offs[:16].T.reshape(-1).astype(np.int64)


E2M1 = np.array([0.0, 0.5, 1.0, 1.5, 2.0, 3.0, 4.0, 6.0, -0.0, -0.5, -1.0, -1.5, -2.0, -3.0, -4.0, -6.0])


def pack_weight(w, fmt):
    k, n = w.shape
    w = f64(np.asarray(w, np.float32).astype(ml_dtypes.bfloat16)).reshape(k // 32, 32, n)
    amax = np.abs(w).max(1)
    if fmt == "e4m3":
        byte = np.frexp(amax)[1] - 1 + 127 - 7
    else:
        mant, ex = np.frexp(amax / 6.0)
        byte = np.where(mant > 0.5, ex, ex - 1) + 127
    byte = np.clip(np.where(amax > 0, byte, 1), 1, 254)
    scaled = (w * np.exp2(127.0 - byte)[:, None, :]).reshape(k, n).astype(np.float32)
    by_word = np.ascontiguousarray(scaled.reshape(k // 512, 128, 4, n).transpose(0, 1, 3, 2))
    if fmt == "e4m3":
        words = by_word.astype(ml_dtypes.float8_e4m3fn).view(np.uint8)
    else:
        c = by_word.astype(ml_dtypes.float4_e2m1fn).view(np.uint8) & 0xF
        words = (c[..., 0::2] | (c[..., 1::2] << 4)).reshape(k // 512, 128, 2 * n)
    return np.ascontiguousarray(words), np.ascontiguousarray(byte.astype(np.uint8).reshape(k // 512, 16, n))


def unpack_weight(words, scales, fmt):
    g, _, n = scales.shape
    words = np.ascontiguousarray(words).reshape(g, 128, n, -1)
    if fmt == "e4m3":
        vals = words.view(ml_dtypes.float8_e4m3fn).astype(np.float64)
    else:
        nib = np.empty((g, 128, n, 4), np.uint8)
        nib[..., 0::2] = words & 0xF
        nib[..., 1::2] = words >> 4
        vals = E2M1[nib]
    vals = vals * np.repeat(np.exp2(scales.astype(np.float64) - 127.0), 8, axis=1)[..., None]
    return vals.transpose(0, 1, 3, 2).reshape(g * 512, n)


def relu(v):
    return np.maximum(v, 0.0)


K, T, E, C, N = 1536, 768, 12, 128, 128
TOP = 4
PAD = 64


def by_expert(wq, xq):
    return np.concatenate([wq[e].T @ xq[:, e * C:(e + 1) * C] for e in range(E)], axis=1)


def setup_inputs():
    n = np.random.standard_normal
    s = mx_kscale(K)[:, None]
    slot_token = np.empty(E * C, np.int64); pos = np.tile(E * C + np.arange(T) % PAD, (TOP, 1)); taken = np.zeros(T, np.int64)
    liked = np.random.randn(T)
    for e in np.random.permutation(E):
        free = np.flatnonzero(taken < TOP); pick = np.random.permutation(free[np.argsort(-(liked[free] + np.random.gumbel(size=free.size)))[:C]]); slot_token[e * C:(e + 1) * C] = pick
        pos[taken[pick], pick] = e * C + np.arange(C); taken[pick] += 1
    g = np.random.uniform(0.2, 0.8, (TOP, T))
    w = [pack_weight(m, "e2m1") for m in n((E, K, N)) / np.sqrt(K) / s[None]]
    return {
        "xT": (n((K, T)) * s).astype(np.float32),
        "w_words": np.stack([m[0] for m in w]),
        "w_scales": np.stack([m[1] for m in w]),
        "b": (0.3 * n((N, E))).astype(np.float32),
        "gate": np.stack([np.tile(r, (N, 1)) for r in g]).astype(np.float32),
        "offs": striped(slot_token),
        "pos1": striped(pos[0]),
        "pos2": striped(pos[1]),
        "pos3": striped(pos[2]),
        "pos4": striped(pos[3]),
    }


def reference(xT, w_words, w_scales, b, gate, offs, pos1, pos2, pos3, pos4):
    idx = unstriped(offs)
    w = np.stack([unpack_weight(w_words[e], w_scales[e], "e2m1") for e in range(E)])
    xq = mxq(f64(xT)[:, idx], 0, "e4m3")
    y = by_expert(w, xq)
    y = relu(y + np.repeat(f64(b), C, axis=1))
    y = np.concatenate([y, np.zeros((N, PAD))], axis=1)
    return sum(f64(gate[r]) * y[:, unstriped(p)] for r, p in enumerate((pos1, pos2, pos3, pos4)))

@@ -1,0 +1,184 @@
+from contextlib import ExitStack
+
+import concourse.mybir as mybir
+from concourse.masks import make_identity
+
+K, T, E, C, N = 1536, 768, 12, 128, 128
+TOP = 4
+PAD = 64
+S = E * C
+FLOPS = 2 * K * N * S
+
+F32 = mybir.dt.float32
+BF16 = mybir.dt.bfloat16
+I32 = mybir.dt.int32
+U32 = mybir.dt.uint32
+U16 = mybir.dt.uint16
+U8 = mybir.dt.uint8
+FP8X4 = mybir.dt.float8_e4m3fn_x4
+FP4X4 = mybir.dt.float4_e2m1fn_x4
+RELU = mybir.ActivationFunctionType.Relu
+MULT = mybir.AluOpType.mult
+ADD = mybir.AluOpType.add
+
+P = 128
+PACK = 4
+PASSES = K // (P * PACK)
+TOK = 256
+SHIFT_ROWS = 112
+
+
+def tile_moe_ecr_lin_relu_kernel(
+    tc, xT, w_words, w_scales, b, gate, offs, pos1, pos2, pos3, pos4, out
+):
+    nc = tc.nc
+    with ExitStack() as ctx:
+        lists = ctx.enter_context(tc.tile_pool(name="lists", bufs=1))
+        keep = ctx.enter_context(tc.tile_pool(name="keep", bufs=1))
+        psum = ctx.enter_context(tc.psum_pool(name="psum", bufs=8))
+
+        offs_t = lists.tile([P, S // 16], U16, name="offs_t")
+        pos_t = [lists.tile([P, T // 16], U16, name="pos_t%d" % r) for r in range(TOP)]
+
+        chunks = [slice(c, c + TOK) for c in range(0, T, TOK)]
+        raw = [[keep.tile([P, PACK, TOK], F32, name="raw%d_%d" % (a, c)) for c in range(len(chunks))] for a in range(PASSES)]
+        grouped = [keep.tile([P, T, PACK], BF16, name="grouped%d" % a, tag="grouped%d" % a, align_bytes=64) for a in range(PASSES)]
+        tok_words = [keep.tile([P, T], U32, name="tok_words%d" % a, align_bytes=64) for a in range(PASSES)]
+        tok_bytes = keep.tile([P, T], U8, name="tok_bytes", tag="late", align_bytes=64)
+        word_cuts = [[0, 4, 8, 12], [0, 4, 8, 12], [0, 4, 8, 11, 12]]
+        byte_cuts = [0, 4, 8, 12]
+        slot_words = [
+            [keep.tile([P, (hi - lo) * C], U32, name="slot_words%d_%d" % (a, lo), align_bytes=64) if (a, lo) != (1, 8) else None for lo, hi in zip(cuts[:-1], cuts[1:])]
+            for a, cuts in enumerate(word_cuts)
+        ]
+        slot_bytes = [
+            [keep.tile([P, (hi - lo) * C], U8, name="slot_bytes%d_%d" % (a, lo), align_bytes=64) for lo, hi in zip(byte_cuts[:-1], byte_cuts[1:])]
+            for a in range(PASSES)
+        ]
+
+        def of_expert(tiles, cuts, e):
+            g = max(i for i, lo in enumerate(cuts) if lo <= e)
+            return tiles[g][:, (e - cuts[g]) * C:(e - cuts[g] + 1) * C]
+
+        w_t = keep.tile([P, E * PASSES, 2 * N], U8, name="w_t", align_bytes=64)
+        ws_t = keep.tile([P, E * PASSES, N], U8, name="ws_t", align_bytes=64)
+        b_t = keep.tile([P, E], F32, name="b_t")
+        gate_first = keep.tile([P, TOP, TOK], F32, name="gate_first")
+        ident = keep.tile([P, P], F32, name="ident")
+        y = keep.tile([P, S + PAD], F32, name="y")
+        zeros = keep.tile([P, PAD], F32, name="zeros")
+
+        for a in range(PASSES):
+            rows = xT[a * 512:(a + 1) * 512, :].rearrange("(p j) t -> p j t", j=PACK)
+            for c, tok in enumerate(chunks):
+                nc.sync.dma_start(out=raw[a][c][:], in_=rows[:, :, tok])
+            if a == 0:
+                nc.sync.dma_start(offs_t[:], offs)
+            if a == 1:
+                nc.sync.dma_start(out=b_t[:], in_=b)
+                for r, pos in enumerate((pos1, pos2, pos3, pos4)):
+                    nc.sync.dma_start(pos_t[r][:], pos)
+
+        nc.vector.memset(zeros[:], 0.0)
+        nc.scalar.activation(out=y[:, S:], in_=zeros[:], func=RELU)
+        nc.gpsimd.memset(tok_bytes[:], 0)
+        make_identity(nc, ident[:])
+        nc.vector.memset(ws_t[:].rearrange("p g n -> p (g n)").bitcast(I32), 0)
+        for a in range(1, PASSES):
+            for plane in slot_bytes[a]:
+                nc.vector.memset(plane[:].bitcast(I32), 0)
+
+        ws_src = w_scales.rearrange("e a q n -> q (e a) n").bitcast(I32)
+        ws_dst = ws_t[:].bitcast(I32)
+        for q in range(4):
+            nc.sync.dma_start(out=ws_dst[32 * q:32 * q + 4, :, :], in_=ws_src[4 * q:4 * q + 4, :, :])
+        w_src = w_words.rearrange("e a p n -> p (e a) n").bitcast(I32)
+        w_dst = w_t[:].bitcast(I32)
+        for g in range(3):
+            nc.sync.dma_start(out=w_dst[:, 12 * g:12 * g + 12, :], in_=w_src[:, 12 * g:12 * g + 12, :])
+        gate_src = gate.rearrange("r n t -> n r t")
+
+        def cast(engine, a, c, lo, hi):
+            dst = grouped[a][:, c * TOK + lo:c * TOK + hi, :].rearrange("p (c i) j -> p c j i", i=4)
+            src = raw[a][c][:, :, lo:hi].rearrange("p j (c i) -> p c j i", i=4)
+            if engine == "vector":
+                nc.vector.tensor_copy(out=dst, in_=src)
+            else:
+                nc.scalar.copy(out=dst, in_=src)
+
+        def quantize(a, tok):
+            nc.vector.quantize_mx(
+                out=tok_words[a][:, tok].bitcast(FP8X4),
+                scales=tok_bytes[4 * a:, tok],
+                in_=grouped[a][:, tok, :].rearrange("p t j -> p (t j)"),
+            )
+
+        def gather(tiles, cuts, g, window):
+            nc.vector.tensor_copy(out=tiles[g][:], in_=window[:].indirect(offs_t[:, cuts[g] * C // 16:cuts[g + 1] * C // 16]))
+
+        for c, tok in enumerate(chunks):
+            cast("scalar", 0, c, 0, 80)
+            cast("vector", 0, c, 80, TOK)
+            quantize(0, tok)
+        for g in range(3):
+            gather(slot_words[0], word_cuts[0], g, tok_words[0])
+        for a in (1, 2):
+            for c, tok in enumerate(chunks):
+                cast("scalar", a, c, 0, TOK)
+                quantize(a, tok)
+        for g in range(3):
+            gather(slot_bytes[0], byte_cuts, g, tok_bytes)
+            for a in (1, 2):
+                nc.sync.dma_start(
+                    out=slot_bytes[a][g][0:SHIFT_ROWS, :].bitcast(I32),
+                    in_=slot_bytes[0][g][4 * a:4 * a + SHIFT_ROWS, :].bitcast(I32),
+                )
+        nc.sync.dma_start(out=gate_first[:], in_=gate_src[:, :, 0:TOK])
+        gate_rest = keep.tile([P, TOP, T - TOK], F32, name="gate_rest", tag="late", align_bytes=64)
+        for lo in range(TOK, T, TOK):
+            nc.sync.dma_start(out=gate_rest[:, :, lo - TOK:lo], in_=gate_src[:, :, lo:lo + TOK])
+        slot_words[1][2] = keep.tile([P, 4 * C], U32, name="slot_words1_8", tag="grouped2", align_bytes=64)
+        for g in range(3):
+            gather(slot_words[1], word_cuts[1], g, tok_words[1])
+
+        for g in range(4):
+            gather(slot_words[2], word_cuts[2], g, tok_words[2])
+            for e in range(word_cuts[2][g], word_cuts[2][g + 1]):
+                slots = slice(e * C, (e + 1) * C)
+                acc = psum.tile([P, C], F32, name="acc")
+                for a in range(PASSES):
+                    nc.tensor.matmul_mx(
+                        out=acc[:],
+                        lhsT=w_t[:, e * PASSES + a, :].bitcast(FP4X4),
+                        lhsT_scale=ws_t[:, e * PASSES + a, :],
+                        rhs=of_expert(slot_words[a], word_cuts[a], e).bitcast(FP8X4),
+                        rhs_scale=of_expert(slot_bytes[a], byte_cuts, e),
+                        start=(a == 0),
+                        stop=(a == PASSES - 1),
+                    )
+                nc.scalar.activation(out=y[:, slots], in_=acc[:], func=RELU, bias=b_t[:, e:e + 1])
+
+        cuts = [0, 256, 512, 640, 768]
+        for c, (lo, hi) in enumerate(zip(cuts[:-1], cuts[1:])):
+            width = hi - lo
+            prod = keep.tile([P, TOP, width], F32, name="prod%d" % c)
+            res = keep.tile([P, width], F32, name="res%d" % c)
+            for r in range(TOP):
+                g = gate_first[:, r, lo:hi] if hi <= TOK else gate_rest[:, r, lo - TOK:hi - TOK]
+                nc.vector.tensor_tensor(prod[:, r, :], y[:].indirect(pos_t[r][:, lo // 16:hi // 16]), g, MULT)
+            if hi == T:
+                half = keep.tile([P, 2, width], F32, name="half")
+                nc.vector.tensor_tensor(half[:], prod[:, 0:2, :], prod[:, 2:4, :], ADD)
+                nc.vector.tensor_tensor(res[:], half[:, 0, :], half[:, 1, :], ADD)
+            else:
+                turned = keep.tile([P, width], F32, name="turned%d" % c)
+                for k in range(0, width, P):
+                    total = psum.tile([P, P], F32, name="acc")
+                    for r in range(TOP):
+                        nc.tensor.matmul(total[:], prod[:, r, k:k + P], ident[:], start=(r == 0), stop=(r == TOP - 1), is_transpose=True)
+                    nc.scalar.copy(out=turned[:, k:k + P], in_=total[:])
+                back = psum.tile([P, width], F32, name="acc")
+                for k in range(0, width, P):
+                    nc.tensor.transpose(back[:, k:k + P], turned[:, k:k + P], ident[:])
+                nc.scalar.copy(out=res[:], in_=back[:])
+            nc.sync.dma_start(out=out[:, lo:hi], in_=res[:])

@@ -24,8 +24,20 @@ ADD = mybir.AluOpType.add
 P = 128
 PACK = 4
 PASSES = K // (P * PACK)
-TOK = 256
 SHIFT_ROWS = 112
+RUN = 4
+X_CUTS = [[0,256,512,640,768],[0,256,512,768],[0,256,512,768]]
+VECTOR_SHARE = [[176,176,88,88],[0,0,0],[0,0,0]]
+W_CUTS = [0,6,12]
+WORD_CUTS = [[0,4,8,12],[0,4,8,10,12],[0,4,8,11,12]]
+BYTE_CUTS = [0, 4, 8, 12]
+SHIFT_CUTS = [0,8,12]
+OUT_CUTS = [0,256,512,640,768]
+GATE_FIRST = 256
+
+
+def spans(cuts):
+    return list(zip(cuts[:-1], cuts[1:]))
 
 
 def tile_moe_ecr_lin_relu_kernel(
@@ -40,110 +52,105 @@ def tile_moe_ecr_lin_relu_kernel(
         offs_t = lists.tile([P, S // 16], U16, name="offs_t")
         pos_t = [lists.tile([P, T // 16], U16, name="pos_t%d" % r) for r in range(TOP)]
 
-        chunks = [slice(c, c + TOK) for c in range(0, T, TOK)]
-        raw = [[keep.tile([P, PACK, TOK], F32, name="raw%d_%d" % (a, c)) for c in range(len(chunks))] for a in range(PASSES)]
+        raw = [[keep.tile([P, PACK, hi - lo], F32, name="raw%d_%d" % (a, lo)) for lo, hi in spans(X_CUTS[a])] for a in range(PASSES)]
         grouped = [keep.tile([P, T, PACK], BF16, name="grouped%d" % a, tag="grouped%d" % a, align_bytes=64) for a in range(PASSES)]
         tok_words = [keep.tile([P, T], U32, name="tok_words%d" % a, align_bytes=64) for a in range(PASSES)]
         tok_bytes = keep.tile([P, T], U8, name="tok_bytes", tag="late", align_bytes=64)
-        word_cuts = [[0, 4, 8, 12], [0, 4, 8, 12], [0, 4, 8, 11, 12]]
-        byte_cuts = [0, 4, 8, 12]
-        slot_words = [
-            [keep.tile([P, (hi - lo) * C], U32, name="slot_words%d_%d" % (a, lo), align_bytes=64) if (a, lo) != (1, 8) else None for lo, hi in zip(cuts[:-1], cuts[1:])]
-            for a, cuts in enumerate(word_cuts)
-        ]
-        slot_bytes = [
-            [keep.tile([P, (hi - lo) * C], U8, name="slot_bytes%d_%d" % (a, lo), align_bytes=64) for lo, hi in zip(byte_cuts[:-1], byte_cuts[1:])]
-            for a in range(PASSES)
-        ]
-
-        def of_expert(tiles, cuts, e):
-            g = max(i for i, lo in enumerate(cuts) if lo <= e)
-            return tiles[g][:, (e - cuts[g]) * C:(e - cuts[g] + 1) * C]
-
+        slot_bytes = [keep.tile([P, S], U8, name="slot_bytes%d" % a, align_bytes=64) for a in range(PASSES)]
         w_t = keep.tile([P, E * PASSES, 2 * N], U8, name="w_t", align_bytes=64)
         ws_t = keep.tile([P, E * PASSES, N], U8, name="ws_t", align_bytes=64)
         b_t = keep.tile([P, E], F32, name="b_t")
-        gate_first = keep.tile([P, TOP, TOK], F32, name="gate_first")
+        gate_first = keep.tile([P, TOP, GATE_FIRST], F32, name="gate_first")
         ident = keep.tile([P, P], F32, name="ident")
         y = keep.tile([P, S + PAD], F32, name="y")
         zeros = keep.tile([P, PAD], F32, name="zeros")
 
+        nc.vector.memset(zeros[:], 0.0)
+        nc.scalar.activation(out=y[:, S:], in_=zeros[:], func=RELU)
+        nc.vector.memset(tok_bytes[:].bitcast(I32), 0)
+        make_identity(nc, ident[:])
+        nc.vector.memset(ws_t[:].rearrange("p g n -> p (g n)").bitcast(I32), 0)
+        for a in range(1, PASSES):
+            nc.vector.memset(slot_bytes[a][:].bitcast(I32), 0)
+
+        ws_src = w_scales.rearrange("e a q n -> q (e a) n").bitcast(I32)
+        ws_dst = ws_t[:].bitcast(I32)
+
+        def load_ws(q):
+            nc.sync.dma_start(out=ws_dst[32 * q:32 * q + 4, :, :], in_=ws_src[4 * q:4 * q + 4, :, :])
+
         for a in range(PASSES):
             rows = xT[a * 512:(a + 1) * 512, :].rearrange("(p j) t -> p j t", j=PACK)
-            for c, tok in enumerate(chunks):
-                nc.sync.dma_start(out=raw[a][c][:], in_=rows[:, :, tok])
-            if a == 0:
-                nc.sync.dma_start(offs_t[:], offs)
+            for c, (lo, hi) in enumerate(spans(X_CUTS[a])):
+                nc.sync.dma_start(out=raw[a][c][:], in_=rows[:, :, lo:hi])
+                if (a, c) == (0, 1):
+                    nc.sync.dma_start(offs_t[:], offs)
             if a == 1:
                 nc.sync.dma_start(out=b_t[:], in_=b)
                 for r, pos in enumerate((pos1, pos2, pos3, pos4)):
                     nc.sync.dma_start(pos_t[r][:], pos)
 
-        nc.vector.memset(zeros[:], 0.0)
-        nc.scalar.activation(out=y[:, S:], in_=zeros[:], func=RELU)
-        nc.gpsimd.memset(tok_bytes[:], 0)
-        make_identity(nc, ident[:])
-        nc.vector.memset(ws_t[:].rearrange("p g n -> p (g n)").bitcast(I32), 0)
-        for a in range(1, PASSES):
-            for plane in slot_bytes[a]:
-                nc.vector.memset(plane[:].bitcast(I32), 0)
-
-        ws_src = w_scales.rearrange("e a q n -> q (e a) n").bitcast(I32)
-        ws_dst = ws_t[:].bitcast(I32)
-        for q in range(4):
-            nc.sync.dma_start(out=ws_dst[32 * q:32 * q + 4, :, :], in_=ws_src[4 * q:4 * q + 4, :, :])
+        for q in range(0, 4):
+            load_ws(q)
         w_src = w_words.rearrange("e a p n -> p (e a) n").bitcast(I32)
         w_dst = w_t[:].bitcast(I32)
-        for g in range(3):
-            nc.sync.dma_start(out=w_dst[:, 12 * g:12 * g + 12, :], in_=w_src[:, 12 * g:12 * g + 12, :])
+        for lo, hi in spans(W_CUTS):
+            nc.sync.dma_start(out=w_dst[:, PASSES * lo:PASSES * hi, :], in_=w_src[:, PASSES * lo:PASSES * hi, :])
         gate_src = gate.rearrange("r n t -> n r t")
 
-        def cast(engine, a, c, lo, hi):
-            dst = grouped[a][:, c * TOK + lo:c * TOK + hi, :].rearrange("p (c i) j -> p c j i", i=4)
-            src = raw[a][c][:, :, lo:hi].rearrange("p j (c i) -> p c j i", i=4)
-            if engine == "vector":
-                nc.vector.tensor_copy(out=dst, in_=src)
-            else:
-                nc.scalar.copy(out=dst, in_=src)
+        def cast(copy, a, c, lo, hi):
+            first = X_CUTS[a][c]
+            dst = grouped[a][:, first + lo:first + hi, :].rearrange("p (c i) j -> p c j i", i=RUN)
+            src = raw[a][c][:, :, lo:hi].rearrange("p j (c i) -> p c j i", i=RUN)
+            copy(out=dst, in_=src)
 
-        def quantize(a, tok):
-            nc.vector.quantize_mx(
-                out=tok_words[a][:, tok].bitcast(FP8X4),
-                scales=tok_bytes[4 * a:, tok],
-                in_=grouped[a][:, tok, :].rearrange("p t j -> p (t j)"),
-            )
-
-        def gather(tiles, cuts, g, window):
-            nc.vector.tensor_copy(out=tiles[g][:], in_=window[:].indirect(offs_t[:, cuts[g] * C // 16:cuts[g + 1] * C // 16]))
-
-        for c, tok in enumerate(chunks):
-            cast("scalar", 0, c, 0, 80)
-            cast("vector", 0, c, 80, TOK)
-            quantize(0, tok)
-        for g in range(3):
-            gather(slot_words[0], word_cuts[0], g, tok_words[0])
-        for a in (1, 2):
-            for c, tok in enumerate(chunks):
-                cast("scalar", a, c, 0, TOK)
-                quantize(a, tok)
-        for g in range(3):
-            gather(slot_bytes[0], byte_cuts, g, tok_bytes)
-            for a in (1, 2):
-                nc.sync.dma_start(
-                    out=slot_bytes[a][g][0:SHIFT_ROWS, :].bitcast(I32),
-                    in_=slot_bytes[0][g][4 * a:4 * a + SHIFT_ROWS, :].bitcast(I32),
+        def cast_and_quantize(a):
+            for c, (lo, hi) in enumerate(spans(X_CUTS[a])):
+                cut = hi - lo - VECTOR_SHARE[a][c]
+                cast(nc.scalar.copy, a, c, 0, cut)
+                if cut < hi - lo:
+                    cast(nc.vector.tensor_copy, a, c, cut, hi - lo)
+                nc.vector.quantize_mx(
+                    out=tok_words[a][:, lo:hi].bitcast(FP8X4),
+                    scales=tok_bytes[4 * a:, lo:hi],
+                    in_=grouped[a][:, lo:hi, :].rearrange("p t j -> p (t j)"),
                 )
-        nc.sync.dma_start(out=gate_first[:], in_=gate_src[:, :, 0:TOK])
-        gate_rest = keep.tile([P, TOP, T - TOK], F32, name="gate_rest", tag="late", align_bytes=64)
-        for lo in range(TOK, T, TOK):
-            nc.sync.dma_start(out=gate_rest[:, :, lo - TOK:lo], in_=gate_src[:, :, lo:lo + TOK])
-        slot_words[1][2] = keep.tile([P, 4 * C], U32, name="slot_words1_8", tag="grouped2", align_bytes=64)
-        for g in range(3):
-            gather(slot_words[1], word_cuts[1], g, tok_words[1])
 
-        for g in range(4):
-            gather(slot_words[2], word_cuts[2], g, tok_words[2])
-            for e in range(word_cuts[2][g], word_cuts[2][g + 1]):
+        def gather(dst, window, lo, hi):
+            nc.vector.tensor_copy(out=dst, in_=window[:].indirect(offs_t[:, lo * C // 16:hi * C // 16]))
+
+        slot_words = {}
+
+        def gather_words(a, lo, hi, tag):
+            words = keep.tile([P, (hi - lo) * C], U32, name="slot_words%d_%d" % (a, lo), tag=tag, align_bytes=64)
+            gather(words[:], tok_words[a], lo, hi)
+            for e in range(lo, hi):
+                slot_words[a, e] = words[:, (e - lo) * C:(e - lo + 1) * C]
+
+        cast_and_quantize(0)
+        for lo, hi in spans(WORD_CUTS[0]):
+            gather_words(0, lo, hi, "words0_%d" % lo)
+        cast_and_quantize(1)
+        cast_and_quantize(2)
+        for lo, hi in spans(BYTE_CUTS):
+            gather(slot_bytes[0][:, lo * C:hi * C], tok_bytes, lo, hi)
+            if hi in SHIFT_CUTS:
+                cols = slice(SHIFT_CUTS[SHIFT_CUTS.index(hi) - 1] * C, hi * C)
+                for a in (1, 2):
+                    nc.scalar.dma_start(
+                        out=slot_bytes[a][0:SHIFT_ROWS, cols].bitcast(I32),
+                        in_=slot_bytes[0][4 * a:4 * a + SHIFT_ROWS, cols].bitcast(I32),
+                    )
+        nc.sync.dma_start(out=gate_first[:], in_=gate_src[:, :, 0:GATE_FIRST])
+        gate_rest = keep.tile([P, TOP, T - GATE_FIRST], F32, name="gate_rest", tag="late", align_bytes=64)
+        for lo, hi in spans([GATE_FIRST, 512, T]):
+            nc.sync.dma_start(out=gate_rest[:, :, lo - GATE_FIRST:hi - GATE_FIRST], in_=gate_src[:, :, lo:hi])
+        for lo, hi in spans(WORD_CUTS[1]):
+            gather_words(1, lo, hi, "grouped2" if hi == E else "words1_%d" % lo)
+
+        for lo, hi in spans(WORD_CUTS[2]):
+            gather_words(2, lo, hi, "words2_%d" % lo)
+            for e in range(lo, hi):
                 slots = slice(e * C, (e + 1) * C)
                 acc = psum.tile([P, C], F32, name="acc")
                 for a in range(PASSES):
@@ -151,20 +158,19 @@ def tile_moe_ecr_lin_relu_kernel(
                         out=acc[:],
                         lhsT=w_t[:, e * PASSES + a, :].bitcast(FP4X4),
                         lhsT_scale=ws_t[:, e * PASSES + a, :],
-                        rhs=of_expert(slot_words[a], word_cuts[a], e).bitcast(FP8X4),
-                        rhs_scale=of_expert(slot_bytes[a], byte_cuts, e),
+                        rhs=slot_words[a, e].bitcast(FP8X4),
+                        rhs_scale=slot_bytes[a][:, slots],
                         start=(a == 0),
                         stop=(a == PASSES - 1),
                     )
                 nc.scalar.activation(out=y[:, slots], in_=acc[:], func=RELU, bias=b_t[:, e:e + 1])
 
-        cuts = [0, 256, 512, 640, 768]
-        for c, (lo, hi) in enumerate(zip(cuts[:-1], cuts[1:])):
+        for c, (lo, hi) in enumerate(spans(OUT_CUTS)):
             width = hi - lo
             prod = keep.tile([P, TOP, width], F32, name="prod%d" % c)
             res = keep.tile([P, width], F32, name="res%d" % c)
             for r in range(TOP):
-                g = gate_first[:, r, lo:hi] if hi <= TOK else gate_rest[:, r, lo - TOK:hi - TOK]
+                g = gate_first[:, r, lo:hi] if hi <= GATE_FIRST else gate_rest[:, r, lo - GATE_FIRST:hi - GATE_FIRST]
                 nc.vector.tensor_tensor(prod[:, r, :], y[:].indirect(pos_t[r][:, lo // 16:hi // 16]), g, MULT)
             if hi == T:
                 half = keep.tile([P, 2, width], F32, name="half")

@@ -25,15 +25,16 @@ P = 128
 PACK = 4
 PASSES = K // (P * PACK)
 SHIFT_ROWS = 112
-RUN = 4
+RUN = 2
 X_CUTS = [[0,256,512,640,768],[0,256,512,768],[0,256,512,768]]
-VECTOR_SHARE = [[176,176,88,88],[0,0,0],[0,0,0]]
-W_CUTS = [0,6,12]
-WORD_CUTS = [[0,4,8,12],[0,4,8,10,12],[0,4,8,11,12]]
+VECTOR_SHARE = [[176,176,88,88],[0,0,0],[0,0,96]]
+Q_CUTS = [[0, 256, 512, 640, 768], [0, 512, 768], [0, 512, 768]]
+W_CUTS = [0,4,8,12]
+WORD_CUTS = [[0,4,8,12],[0,4,8,12],[0,4,8,11,12]]
 BYTE_CUTS = [0, 4, 8, 12]
-SHIFT_CUTS = [0,8,12]
-OUT_CUTS = [0,256,512,640,768]
-GATE_FIRST = 256
+SHIFT_CUTS = [0,4,8,12]
+OUT_CUTS = [0,384,640,768]
+GATE_CUT = 384
 
 
 def spans(cuts):
@@ -60,7 +61,6 @@ def tile_moe_ecr_lin_relu_kernel(
         w_t = keep.tile([P, E * PASSES, 2 * N], U8, name="w_t", align_bytes=64)
         ws_t = keep.tile([P, E * PASSES, N], U8, name="ws_t", align_bytes=64)
         b_t = keep.tile([P, E], F32, name="b_t")
-        gate_first = keep.tile([P, TOP, GATE_FIRST], F32, name="gate_first")
         ident = keep.tile([P, P], F32, name="ident")
         y = keep.tile([P, S + PAD], F32, name="y")
         zeros = keep.tile([P, PAD], F32, name="zeros")
@@ -110,11 +110,13 @@ def tile_moe_ecr_lin_relu_kernel(
                 cast(nc.scalar.copy, a, c, 0, cut)
                 if cut < hi - lo:
                     cast(nc.vector.tensor_copy, a, c, cut, hi - lo)
-                nc.vector.quantize_mx(
-                    out=tok_words[a][:, lo:hi].bitcast(FP8X4),
-                    scales=tok_bytes[4 * a:, lo:hi],
-                    in_=grouped[a][:, lo:hi, :].rearrange("p t j -> p (t j)"),
-                )
+                if hi in Q_CUTS[a]:
+                    tok = slice(Q_CUTS[a][Q_CUTS[a].index(hi) - 1], hi)
+                    nc.vector.quantize_mx(
+                        out=tok_words[a][:, tok].bitcast(FP8X4),
+                        scales=tok_bytes[4 * a:, tok],
+                        in_=grouped[a][:, tok, :].rearrange("p t j -> p (t j)"),
+                    )
 
         def gather(dst, window, lo, hi):
             nc.vector.tensor_copy(out=dst, in_=window[:].indirect(offs_t[:, lo * C // 16:hi * C // 16]))
@@ -137,18 +139,20 @@ def tile_moe_ecr_lin_relu_kernel(
             if hi in SHIFT_CUTS:
                 cols = slice(SHIFT_CUTS[SHIFT_CUTS.index(hi) - 1] * C, hi * C)
                 for a in (1, 2):
-                    nc.scalar.dma_start(
+                    nc.sync.dma_start(
                         out=slot_bytes[a][0:SHIFT_ROWS, cols].bitcast(I32),
                         in_=slot_bytes[0][4 * a:4 * a + SHIFT_ROWS, cols].bitcast(I32),
                     )
-        nc.sync.dma_start(out=gate_first[:], in_=gate_src[:, :, 0:GATE_FIRST])
-        gate_rest = keep.tile([P, TOP, T - GATE_FIRST], F32, name="gate_rest", tag="late", align_bytes=64)
-        for lo, hi in spans([GATE_FIRST, 512, T]):
-            nc.sync.dma_start(out=gate_rest[:, :, lo - GATE_FIRST:hi - GATE_FIRST], in_=gate_src[:, :, lo:hi])
-        for lo, hi in spans(WORD_CUTS[1]):
-            gather_words(1, lo, hi, "grouped2" if hi == E else "words1_%d" % lo)
+        gate_t = keep.tile([P, TOP, T], F32, name="gate_t", tag="late", align_bytes=64)
+        for r in (0, 2):
+            nc.sync.dma_start(out=gate_t[:, r:r + 2, 0:GATE_CUT], in_=gate_src[:, r:r + 2, 0:GATE_CUT])
+        nc.sync.dma_start(out=gate_t[:, :, GATE_CUT:], in_=gate_src[:, :, GATE_CUT:])
+        for lo, hi in spans(WORD_CUTS[1])[:-1]:
+            gather_words(1, lo, hi, "words1_%d" % lo)
 
         for lo, hi in spans(WORD_CUTS[2]):
+            if lo == WORD_CUTS[1][-2]:
+                gather_words(1, lo, E, "grouped2")
             gather_words(2, lo, hi, "words2_%d" % lo)
             for e in range(lo, hi):
                 slots = slice(e * C, (e + 1) * C)
@@ -169,14 +173,21 @@ def tile_moe_ecr_lin_relu_kernel(
             width = hi - lo
             prod = keep.tile([P, TOP, width], F32, name="prod%d" % c)
             res = keep.tile([P, width], F32, name="res%d" % c)
-            for r in range(TOP):
-                g = gate_first[:, r, lo:hi] if hi <= GATE_FIRST else gate_rest[:, r, lo - GATE_FIRST:hi - GATE_FIRST]
-                nc.vector.tensor_tensor(prod[:, r, :], y[:].indirect(pos_t[r][:, lo // 16:hi // 16]), g, MULT)
+
+            def fetch(r):
+                nc.vector.tensor_tensor(prod[:, r, :], y[:].indirect(pos_t[r][:, lo // 16:hi // 16]), gate_t[:, r, lo:hi], MULT)
+
             if hi == T:
-                half = keep.tile([P, 2, width], F32, name="half")
-                nc.vector.tensor_tensor(half[:], prod[:, 0:2, :], prod[:, 2:4, :], ADD)
-                nc.vector.tensor_tensor(res[:], half[:, 0, :], half[:, 1, :], ADD)
+                part = keep.tile([P, 2, width], F32, name="part")
+                for r in range(3):
+                    fetch(r)
+                nc.vector.tensor_tensor(part[:, 0, :], prod[:, 0, :], prod[:, 1, :], ADD)
+                fetch(3)
+                nc.vector.tensor_tensor(part[:, 1, :], part[:, 0, :], prod[:, 2, :], ADD)
+                nc.vector.tensor_tensor(res[:], part[:, 1, :], prod[:, 3, :], ADD)
             else:
+                for r in range(TOP):
+                    fetch(r)
                 turned = keep.tile([P, width], F32, name="turned%d" % c)
                 for k in range(0, width, P):
                     total = psum.tile([P, P], F32, name="acc")

from contextlib import ExitStack

import concourse.mybir as mybir
from concourse.masks import make_identity

K, T, E, C, N = 1536, 768, 12, 128, 128
TOP = 4
PAD = 64
S = E * C
FLOPS = 2 * K * N * S

F32 = mybir.dt.float32
BF16 = mybir.dt.bfloat16
I32 = mybir.dt.int32
U32 = mybir.dt.uint32
U16 = mybir.dt.uint16
U8 = mybir.dt.uint8
FP8X4 = mybir.dt.float8_e4m3fn_x4
FP4X4 = mybir.dt.float4_e2m1fn_x4
RELU = mybir.ActivationFunctionType.Relu
MULT = mybir.AluOpType.mult
ADD = mybir.AluOpType.add

P = 128
PACK = 4
PASSES = K // (P * PACK)
SHIFT_ROWS = 112
RUN = 2
X_CUTS = [[0,256,512,640,768],[0,256,512,768],[0,256,512,768]]
VECTOR_SHARE = [[176,176,88,88],[0,0,0],[0,0,96]]
Q_CUTS = [[0, 256, 512, 640, 768], [0, 512, 768], [0, 512, 768]]
W_CUTS = [0,4,8,12]
WORD_CUTS = [[0,4,8,12],[0,4,8,12],[0,4,8,11,12]]
BYTE_CUTS = [0, 4, 8, 12]
SHIFT_CUTS = [0,4,8,12]
OUT_CUTS = [0,384,640,768]
GATE_CUT = 384


def spans(cuts):
    return list(zip(cuts[:-1], cuts[1:]))


def tile_moe_ecr_lin_relu_kernel(
    tc, xT, w_words, w_scales, b, gate, offs, pos1, pos2, pos3, pos4, out
):
    nc = tc.nc
    with ExitStack() as ctx:
        lists = ctx.enter_context(tc.tile_pool(name="lists", bufs=1))
        keep = ctx.enter_context(tc.tile_pool(name="keep", bufs=1))
        psum = ctx.enter_context(tc.psum_pool(name="psum", bufs=8))

        offs_t = lists.tile([P, S // 16], U16, name="offs_t")
        pos_t = [lists.tile([P, T // 16], U16, name="pos_t%d" % r) for r in range(TOP)]

        raw = [[keep.tile([P, PACK, hi - lo], F32, name="raw%d_%d" % (a, lo)) for lo, hi in spans(X_CUTS[a])] for a in range(PASSES)]
        grouped = [keep.tile([P, T, PACK], BF16, name="grouped%d" % a, tag="grouped%d" % a, align_bytes=64) for a in range(PASSES)]
        tok_words = [keep.tile([P, T], U32, name="tok_words%d" % a, align_bytes=64) for a in range(PASSES)]
        tok_bytes = keep.tile([P, T], U8, name="tok_bytes", tag="late", align_bytes=64)
        slot_bytes = [keep.tile([P, S], U8, name="slot_bytes%d" % a, align_bytes=64) for a in range(PASSES)]
        w_t = keep.tile([P, E * PASSES, 2 * N], U8, name="w_t", align_bytes=64)
        ws_t = keep.tile([P, E * PASSES, N], U8, name="ws_t", align_bytes=64)
        b_t = keep.tile([P, E], F32, name="b_t")
        ident = keep.tile([P, P], F32, name="ident")
        y = keep.tile([P, S + PAD], F32, name="y")
        zeros = keep.tile([P, PAD], F32, name="zeros")

        nc.vector.memset(zeros[:], 0.0)
        nc.scalar.activation(out=y[:, S:], in_=zeros[:], func=RELU)
        nc.vector.memset(tok_bytes[:].bitcast(I32), 0)
        make_identity(nc, ident[:])
        nc.vector.memset(ws_t[:].rearrange("p g n -> p (g n)").bitcast(I32), 0)
        for a in range(1, PASSES):
            nc.vector.memset(slot_bytes[a][:].bitcast(I32), 0)

        ws_src = w_scales.rearrange("e a q n -> q (e a) n").bitcast(I32)
        ws_dst = ws_t[:].bitcast(I32)

        def load_ws(q):
            nc.sync.dma_start(out=ws_dst[32 * q:32 * q + 4, :, :], in_=ws_src[4 * q:4 * q + 4, :, :])

        for a in range(PASSES):
            rows = xT[a * 512:(a + 1) * 512, :].rearrange("(p j) t -> p j t", j=PACK)
            for c, (lo, hi) in enumerate(spans(X_CUTS[a])):
                nc.sync.dma_start(out=raw[a][c][:], in_=rows[:, :, lo:hi])
                if (a, c) == (0, 1):
                    nc.sync.dma_start(offs_t[:], offs)
            if a == 1:
                nc.sync.dma_start(out=b_t[:], in_=b)
                for r, pos in enumerate((pos1, pos2, pos3, pos4)):
                    nc.sync.dma_start(pos_t[r][:], pos)

        for q in range(0, 4):
            load_ws(q)
        w_src = w_words.rearrange("e a p n -> p (e a) n").bitcast(I32)
        w_dst = w_t[:].bitcast(I32)
        for lo, hi in spans(W_CUTS):
            nc.sync.dma_start(out=w_dst[:, PASSES * lo:PASSES * hi, :], in_=w_src[:, PASSES * lo:PASSES * hi, :])
        gate_src = gate.rearrange("r n t -> n r t")

        def cast(copy, a, c, lo, hi):
            first = X_CUTS[a][c]
            dst = grouped[a][:, first + lo:first + hi, :].rearrange("p (c i) j -> p c j i", i=RUN)
            src = raw[a][c][:, :, lo:hi].rearrange("p j (c i) -> p c j i", i=RUN)
            copy(out=dst, in_=src)

        def cast_and_quantize(a):
            for c, (lo, hi) in enumerate(spans(X_CUTS[a])):
                cut = hi - lo - VECTOR_SHARE[a][c]
                cast(nc.scalar.copy, a, c, 0, cut)
                if cut < hi - lo:
                    cast(nc.vector.tensor_copy, a, c, cut, hi - lo)
                if hi in Q_CUTS[a]:
                    tok = slice(Q_CUTS[a][Q_CUTS[a].index(hi) - 1], hi)
                    nc.vector.quantize_mx(
                        out=tok_words[a][:, tok].bitcast(FP8X4),
                        scales=tok_bytes[4 * a:, tok],
                        in_=grouped[a][:, tok, :].rearrange("p t j -> p (t j)"),
                    )

        def gather(dst, window, lo, hi):
            nc.vector.tensor_copy(out=dst, in_=window[:].indirect(offs_t[:, lo * C // 16:hi * C // 16]))

        slot_words = {}

        def gather_words(a, lo, hi, tag):
            words = keep.tile([P, (hi - lo) * C], U32, name="slot_words%d_%d" % (a, lo), tag=tag, align_bytes=64)
            gather(words[:], tok_words[a], lo, hi)
            for e in range(lo, hi):
                slot_words[a, e] = words[:, (e - lo) * C:(e - lo + 1) * C]

        cast_and_quantize(0)
        for lo, hi in spans(WORD_CUTS[0]):
            gather_words(0, lo, hi, "words0_%d" % lo)
        cast_and_quantize(1)
        cast_and_quantize(2)
        for lo, hi in spans(BYTE_CUTS):
            gather(slot_bytes[0][:, lo * C:hi * C], tok_bytes, lo, hi)
            if hi in SHIFT_CUTS:
                cols = slice(SHIFT_CUTS[SHIFT_CUTS.index(hi) - 1] * C, hi * C)
                for a in (1, 2):
                    nc.sync.dma_start(
                        out=slot_bytes[a][0:SHIFT_ROWS, cols].bitcast(I32),
                        in_=slot_bytes[0][4 * a:4 * a + SHIFT_ROWS, cols].bitcast(I32),
                    )
        gate_t = keep.tile([P, TOP, T], F32, name="gate_t", tag="late", align_bytes=64)
        for r in (0, 2):
            nc.sync.dma_start(out=gate_t[:, r:r + 2, 0:GATE_CUT], in_=gate_src[:, r:r + 2, 0:GATE_CUT])
        nc.sync.dma_start(out=gate_t[:, :, GATE_CUT:], in_=gate_src[:, :, GATE_CUT:])
        for lo, hi in spans(WORD_CUTS[1])[:-1]:
            gather_words(1, lo, hi, "words1_%d" % lo)

        for lo, hi in spans(WORD_CUTS[2]):
            if lo == WORD_CUTS[1][-2]:
                gather_words(1, lo, E, "grouped2")
            gather_words(2, lo, hi, "words2_%d" % lo)
            for e in range(lo, hi):
                slots = slice(e * C, (e + 1) * C)
                acc = psum.tile([P, C], F32, name="acc")
                for a in range(PASSES):
                    nc.tensor.matmul_mx(
                        out=acc[:],
                        lhsT=w_t[:, e * PASSES + a, :].bitcast(FP4X4),
                        lhsT_scale=ws_t[:, e * PASSES + a, :],
                        rhs=slot_words[a, e].bitcast(FP8X4),
                        rhs_scale=slot_bytes[a][:, slots],
                        start=(a == 0),
                        stop=(a == PASSES - 1),
                    )
                nc.scalar.activation(out=y[:, slots], in_=acc[:], func=RELU, bias=b_t[:, e:e + 1])

        for c, (lo, hi) in enumerate(spans(OUT_CUTS)):
            width = hi - lo
            prod = keep.tile([P, TOP, width], F32, name="prod%d" % c)
            res = keep.tile([P, width], F32, name="res%d" % c)

            def fetch(r):
                nc.vector.tensor_tensor(prod[:, r, :], y[:].indirect(pos_t[r][:, lo // 16:hi // 16]), gate_t[:, r, lo:hi], MULT)

            if hi == T:
                part = keep.tile([P, 2, width], F32, name="part")
                for r in range(3):
                    fetch(r)
                nc.vector.tensor_tensor(part[:, 0, :], prod[:, 0, :], prod[:, 1, :], ADD)
                fetch(3)
                nc.vector.tensor_tensor(part[:, 1, :], part[:, 0, :], prod[:, 2, :], ADD)
                nc.vector.tensor_tensor(res[:], part[:, 1, :], prod[:, 3, :], ADD)
            else:
                for r in range(TOP):
                    fetch(r)
                turned = keep.tile([P, width], F32, name="turned%d" % c)
                for k in range(0, width, P):
                    total = psum.tile([P, P], F32, name="acc")
                    for r in range(TOP):
                        nc.tensor.matmul(total[:], prod[:, r, k:k + P], ident[:], start=(r == 0), stop=(r == TOP - 1), is_transpose=True)
                    nc.scalar.copy(out=turned[:, k:k + P], in_=total[:])
                back = psum.tile([P, width], F32, name="acc")
                for k in range(0, width, P):
                    nc.tensor.transpose(back[:, k:k + P], turned[:, k:k + P], ident[:])
                nc.scalar.copy(out=res[:], in_=back[:])
            nc.sync.dma_start(out=out[:, lo:hi], in_=res[:])
